import numpy as np, ml_dtypes
CORES = [6,15,38,47]
N = 4
import mx_ref
BF = ml_dtypes.bfloat16
def cols(t, e):
    v = np.concatenate([t.reshape(128, -1, 4), np.zeros((128, 1, 4), BF)], axis=1)
    return np.ascontiguousarray(v[:, e]).reshape(128, -1)
def cut(t, i, w=512):
    return t[:, w * i:w * i + w]
def f(rng, *shape):
    return mx_ref.flush((rng.standard_normal(shape, dtype=np.float32) * np.exp2(rng.integers(-2, 3, shape[:-1] + (1,)))).astype(BF))
def wide(rng, *shape, cols=0):
    v = rng.standard_normal(shape, dtype=np.float32) * np.exp2(rng.integers(-12, 13, shape)).astype(np.float32)
    if cols: v *= np.repeat(np.exp2(rng.integers(-cols, cols + 1, shape[:-2] + (1, shape[-1] // 4))) * (rng.random(shape[:-2] + (1, shape[-1] // 4)) > 0.0625), 4, axis=-1).astype(np.float32)
    return mx_ref.flush(v.astype(BF))
P, K, R, O = 256, 64, 6, 2
PART = [1, 2, 1, 2, 1, 2]
def scores(c, qt):
    k = mx_ref.quantize(np.concatenate([qt[r][:, :4 * R] for r in range(N)], axis=1))
    s = [mx_ref.matmul(mx_ref.quantize(cut(c[q], i)), k) for q in range(N) for i in range(P // 128)]
    return np.concatenate(s).reshape(N * P, N, R)
def play(s):
    held, use, out = np.arange(N * P).reshape(N, P), np.zeros((N, P), np.float32), []
    for t in range(R):
        left = []
        for r in range(N):
            v = s[held[r], r, t]
            use[r] = use[r] + v * v
            left.append(np.argsort(use[r], kind="stable")[:K])
        new = held.copy()
        for r in range(N):
            p = r ^ PART[t]
            new[r, left[r]] = held[p, left[p]]
            use[r, left[r]] = 0
        held = new
        out.append(held)
    return np.stack(out)
def fit(s):
    a = np.abs(s)
    return bool(np.isfinite(a).all() and ((a == 0) | (a >= 2.0 ** -60) & (a <= 2.0 ** 60)).all())
def times(t, v):
    return mx_ref.flush((t.astype(np.float32) * np.asarray(v, np.float32)).astype(BF))
def plain(rng):
    q = np.array(f(rng, N, 128, 512))
    q[:, :, 4 * R:] = 0
    return {"c": f(rng, N, 128, 4 * P), "qt": q, "w": f(rng, N, 128, 512 * O)}
def first(make, good=None):
    for i in range(50):
        d = make()
        s = scores(d["c"], d["qt"])
        if fit(s) and (good is None or good(s)): return d
    raise RuntimeError("no draw of 50 is fit")
def athome(s):
    h, a = play(s), np.ones((N, R + 1, P), bool)
    for r in range(N):
        for t in range(R): a[r, t + 1] = np.isin(np.arange(P * r, P * r + P), h[t, r])
    return a
def setup_inputs(rng):
    return first(lambda: plain(rng))
def setup_inputs_sides(rng):
    top = np.arange(128) < 64
    def make():
        d = plain(rng)
        half = np.stack([rng.permutation(P) < P // 2 for r in range(N)])
        d["c"] = times(d["c"], np.repeat(half[:, None, :] == top[None, :, None], 4, axis=2))
        for t in range(R):
            g = np.where(top == (PART[t] == 1), 1.0, 2.0 ** -6) * 4.0 ** t
            d["qt"][:, :, 4 * t:4 * t + 4] = times(d["qt"][:, :, 4 * t:4 * t + 4], g[None, :, None])
        return d
    def good(s):
        a = athome(s)
        return bool((~a[:, :-1] & a[:, 1:]).any(axis=(1, 2)).all())
    return first(make, good)
def setup_inputs_ties(rng):
    def make():
        d = plain(rng)
        d["c"] = np.stack([times(cols(d["c"][r], rng.integers(0, 6, P)), np.repeat(1 - 2 * rng.integers(0, 2, P), 4)) for r in range(N)])
        return d
    def good(s):
        for r in range(N):
            v = s[P * r:P * r + P, r, 0]
            u = np.sort(v * v)
            if u[K - 1] != u[K]: return False
        return True
    return first(make, good)
def setup_inputs_shrink(rng):
    low = np.arange(N) >= N - N // 4
    def make():
        d = plain(rng)
        size = np.exp2(np.where(low, -30.0, 23.0)[:, None] + 2 * rng.random((N, P))) * (1 - 2 * rng.integers(0, 2, (N, P)))
        d["c"] = ((1 + rng.random((N, 128, 4 * P))) * np.repeat(size, 4, axis=1)[:, None, :]).astype(np.float32).astype(BF)
        on = ~low[:, None] | np.stack([rng.permutation(128) < 2 for r in range(N)])
        for t in range(R):
            g = np.exp2(np.where(low, 8.0 * (R - 1 - t) - 30.0, 21.0 - 8.0 * t))
            d["qt"][:, :, 4 * t:4 * t + 4] = ((1 + rng.random((N, 128, 4))) * (g[:, None] * on)[:, :, None]).astype(np.float32).astype(BF)
        return d
    def good(s):
        h, a, b = play(s), np.zeros(N, bool), np.zeros(N, bool)
        for r in range(N):
            at, use, since = np.arange(P * r, P * r + P), np.zeros(P, np.float32), np.zeros(P, int)
            if low[r] and np.abs(s[at, r, R - 1]).max() > 2.0 ** -50 or not low[r] and np.abs(s[at, r, 0]).min() < 2.0 ** 50: return False
            for t in range(R):
                v = s[at, r]
                use = use + v[:, t] * v[:, t]
                sums = np.concatenate([np.zeros((P, 1), np.float32), np.cumsum(v * v, axis=1)], axis=1)
                diff = sums[:, t + 1] - sums[np.arange(P), since]
                a[r] |= (np.argsort(use, kind="stable")[:K] != np.argsort(diff, kind="stable")[:K]).any()
                b[r] |= np.sort(use)[K - 1] > 1e30
                moved = h[t, r] != at
                at = h[t, r]
                use[moved] = 0
                since[moved] = t + 1
        return bool(2 * a.sum() > N and 2 * b.sum() > N)
    return first(make, good)
def setup_inputs_turn(rng):
    on = (np.arange(128) // (128 // N))[None, :] == np.arange(N)[:, None]
    def make():
        d = plain(rng)
        d["c"] = times(d["c"], np.where(on, 2.0 ** -8, 1.0)[:, :, None])
        d["qt"] = times(d["qt"], on[:, :, None])
        return d
    return first(make, lambda s: bool((~athome(s)).any(axis=1).all()))
def setup_inputs_spread(rng):
    return first(lambda: {**plain(rng), "c": wide(rng, N, 128, 4 * P, cols=6)})
def check_inputs(d):
    b = []
    for k in ("c", "qt", "w"):
        v = np.abs(d[k].astype(np.float32))
        if not (np.isfinite(v).all() and ((v == 0) | (v >= 2.0 ** -30) & (v <= 2.0 ** 30)).all()): b.append("a value of " + k)
    if (d["qt"][:, :, 4 * R:].astype(np.float32) != 0).any(): b.append("qt has numbers behind its first R columns")
    if not b and not fit(scores(d["c"], d["qt"])): b.append("a score")
    return b
def reference(c, qt, w):
    held = play(scores(c, qt))
    every = np.concatenate([c[q] for q in range(N)], axis=1)
    y = np.zeros((N, 128, R * O * P), np.float32)
    for r in range(N):
        u, at = np.unique(held[:, r].reshape(-1), return_inverse=True)
        at = at.reshape(R, P)
        q = mx_ref.quantize(cols(every, np.concatenate([u, np.full(-len(u) % 4, -1)])))
        for o in range(O):
            z = mx_ref.matmul(mx_ref.quantize(cut(w[r], o)), q)
            for t in range(R):
                i = (t * O + o) * P
                y[r, :, i:i + P] = z[:, at[t]]
    return {"y": y}

@@ -1,0 +1,336 @@
+from concourse.bass import DstId, RemoteDMATransfer
+from concourse.mybir import dt, AluOpType, ActivationFunctionType
+
+P, K, R, O = 256, 64, 6, 2
+PART = [1, 2, 1, 2, 1, 2]
+W = P + K
+CODE, PLANE = "float8_e4m3fn_x4", "uint8"
+
+SCRATCH = {
+    "cin": ("sbuf", [128, 4 * P], "bfloat16"),
+    "qin": ("sbuf", [128, 512], "bfloat16"),
+    "win": ("sbuf", [128, 512 * O], "bfloat16"),
+    "qk": ("sbuf", [128, 128], CODE), "qks": ("sbuf", [128, 128], PLANE),
+    "qr": ("sbuf", [128, 128 * R], CODE), "qrs": ("sbuf", [128, 128 * R], PLANE),
+    "wk": ("sbuf", [128, 128 * O], CODE), "wks": ("sbuf", [128, 128 * O], PLANE),
+    "far": ("sbuf", [128, P], CODE), "fars": ("sbuf", [128, P], PLANE),
+    "offq": ("sbuf", [128, 8 * R], "uint16"),
+    "lst0": ("sbuf", [128, K // 16], "uint16"),
+    "lland": ("sbuf", [128, K // 16], "uint16"),
+    "lst": ("sbuf", [128, R * K // 16], "uint16"),
+    "mrg": ("sbuf", [128, R * P // 16], "uint16"),
+    "U": ("sbuf", [128, R * P], "float32"),
+    "V": ("sbuf", [128, R * W], "float32"),
+    "sqn": ("sbuf", [128, P], "float32"),
+    "uc": ("sbuf", [128, 2], "float32"),
+    "us": ("sbuf", [128, 2], "float32"),
+    "X": ("sbuf", [128, 832], "bfloat16"),
+    "G": ("sbuf", [128, 832], "bfloat16"),
+    "SO": ("sbuf", [128, 832], "bfloat16"),
+    "RT": ("sbuf", [128, 64], "bfloat16"),
+    "RB": ("sbuf", [128, P], "bfloat16"),
+    "NE": ("sbuf", [128, 4 * P], "bfloat16"),
+    "LO": ("sbuf", [128, 4 * P], "bfloat16"),
+    "tab": ("sbuf", [128, 4 * P], "bfloat16"),
+    "mk": ("sbuf", [128, P], "bfloat16"),
+    "mx16": ("sbuf", [128, P], "bfloat16"),
+    "mo": ("sbuf", [128, P], "bfloat16"),
+    "gs": ("sbuf", [128, P], "bfloat16"),
+    "ma": ("sbuf", [128, 16], "float32"),
+    "mb": ("sbuf", [128, 16], "float32"),
+    "mc": ("sbuf", [128, 16], "float32"),
+    "md": ("sbuf", [128, 16], "float32"),
+    "fc": ("sbuf", [128, 16], "float32"),
+    "tg": ("sbuf", [128, 4], "bfloat16"),
+    "i16": ("sbuf", [128, 16], "int32"),
+    "ip": ("sbuf", [128, 1], "int32"),
+    "ipm": ("sbuf", [128, 1], "int32"),
+    "idf": ("sbuf", [128, 1], "float32"),
+    "ij": ("sbuf", [128, P], "int32"),
+    "yw": ("sbuf", [128, (R + 1) * O * W], "float32"),
+    "pc": ("psum", [128, 1024], "float32"),
+    "pa": ("psum", [128, 512], "float32"),
+    "pr": ("psum", [128, 512], "float32"),
+    "py": ("psum", [128, 512 * O], "float32"),
+}
+for _t in range(R):
+    SCRATCH["H%d" % _t] = ("sbuf", [128, P], CODE)
+    SCRATCH["H%ds" % _t] = ("sbuf", [128, P], PLANE)
+    SCRATCH["M%d" % _t] = ("sbuf", [128, W], CODE)
+    SCRATCH["M%ds" % _t] = ("sbuf", [128, W], PLANE)
+    if _t:
+        SCRATCH["S%d" % _t] = ("sbuf", [128, K], CODE)
+        SCRATCH["S%ds" % _t] = ("sbuf", [128, K], PLANE)
+SEMAPHORES = ["sv", "ss", "sp", "sg", "ldc", "ldq", "ldw", "loc", "arl", "sty"]
+for _t in range(R):
+    SEMAPHORES += ["cp%d" % _t, "arc%d" % _t, "ars%d" % _t]
+
+
+def rank_program(g, core, T, topo):
+    rank = T.rank_of(core)
+    if rank is None:
+        return
+    A, F = AluOpType, ActivationFunctionType
+    vec, act, ten, syn = g.vector, g.scalar, g.tensor, g.sync
+    queue = {"v": vec, "s": act, "p": ten, "g": g, "y": syn}
+    count = {"v": 0, "s": 0, "p": 0, "g": 0}
+    own = {"v": "sv", "s": "ss", "p": "sp", "g": "sg"}
+    seen = {}
+    sent = [0]
+
+    def wait(q, *deps):
+        top = {}
+        for d in deps:
+            if d is not None:
+                top[d[0]] = max(top.get(d[0], 0), d[1])
+        for s in top:
+            if seen.get((q, s), 0) < top[s]:
+                queue[q].wait_ge(T.sem[s], top[s])
+                seen[(q, s)] = top[s]
+
+    def done(q, ins):
+        count[q] += 1
+        ins.then_inc(T.sem[own[q]], 1)
+        return (own[q], count[q])
+
+    def send(out_ap, in_ap, sem, dst):
+        rid, pid = topo.addr(dst)[:2]
+        g.remote_dma(out_ap=out_ap, in_ap=in_ap, remote_sem=T.sem[sem], local_sem=T.sem["loc"], pid=pid, routing_id=rid, dma_engine_mask=topo.mask(core, dst))
+        sent[0] += len(topo.engines(core, dst))
+
+    def by(t):
+        return len(topo.engines(T.cores[rank ^ PART[t]], core))
+
+    def u8(v):
+        return v.bitcast(dt.uint8)
+
+    def pick(out, win, a, b, c, d, off, deps):
+        wait("v", *deps)
+        return done("v", vec.tensor_copy(T[out][:, a:b].bitcast(dt.uint32), T[win][:, c:d].bitcast(dt.uint32).indirect(off)))
+
+    def picks(out, win, a, b, c, d, off, deps):
+        wait("s", *deps)
+        return done("s", act.activation(T[out][:, a:b], T[win][:, c:d].indirect(off), F.Copy))
+
+    def mm(out, n, st, a, mv, b, deps):
+        wait("p", *deps)
+        return done("p", ten.matmul_mx(out, T[st][:, a:a + 128], T[st + "s"][:, a:a + 128], T[mv][:, b:b + n], T[mv + "s"][:, b:b + n], True, True))
+
+    def fill(ap, x, *deps):
+        wait("v", *deps)
+        return done("v", vec.memset(ap, x))
+
+    def ts(out, in0, s1, s2, op0, op1, *deps):
+        wait("v", *deps)
+        if op1 is None:
+            return done("v", vec.tensor_scalar(out, in0, s1, None, op0))
+        return done("v", vec.tensor_scalar(out, in0, s1, s2, op0, op1))
+
+    def tt(out, in0, in1, op, *deps):
+        wait("v", *deps)
+        return done("v", vec.tensor_tensor(out, in0, in1, op))
+
+    def func(out, in_, f, *deps):
+        wait("s", *deps)
+        return done("s", act.activation(out, in_, f))
+
+    act.dma_start(T.qin[:], T.qt[:]).then_inc(T.sem.ldq, 16)
+    syn.dma_start(T.cin[:], T.c[:]).then_inc(T.sem.ldc, 16)
+    syn.dma_start(T.win[:], T.w[:]).then_inc(T.sem.ldw, 16)
+    toff = [fill(T.offq[:, 0:8], 0)]
+    tg1 = fill(T.G[:], 1.0)
+    ti1 = done("g", g.iota(T.ip[:], [[1, 1]], 0, 1))
+    ti2 = done("g", g.iota(T.i16[:], [[16, 16]], 0, 1))
+    wait("g", tg1)
+    tk = None
+    for h in range(2):
+        v = T.G[:, 416 * h:416 * h + 128]
+        tk = done("g", g.affine_select(v, v, [[-1, 128]], A.not_equal, 0.0, 0, 1))
+    ti3 = done("g", g.iota(T.ij[:], [[0, 16], [1, 16]], 0, 0))
+    for h in range(2):
+        fill(T.G[:, 416 * h + 128:416 * h + 129], -1.0, tg1)
+        fill(T.X[:, 416 * h + 384:416 * h + 416], 0.0)
+    tcon = fill(T.SO[:, 800:832], 0.0)
+    for t in range(1, R):
+        toff.append(fill(T.offq[:, 8 * t:8 * t + 8], t))
+
+    wait("v", ("ldq", 16))
+    tq = done("v", vec.quantize_mx(T.qk[:], T.qks[:], T.qin[:]))
+    trc, trs = [None] * R, [None] * R
+
+    def off(t):
+        return T.offq[:, 8 * t:8 * t + 8]
+
+    trc[0] = pick("qr", "qk", 0, 128, 0, 128, off(0), (tq, toff[0]))
+    trs[0] = picks("qrs", "qks", 0, 128, 0, 128, off(0), (tq, toff[0]))
+    wait("v", ("ldc", 16))
+    hc = hs = done("v", vec.quantize_mx(T.H0[:], T.H0s[:], T.cin[:]))
+
+    dst = T.cores[rank ^ PART[0]]
+    wait("g", hc)
+    send(u8(T.far[:]), u8(T.H0[:]), "arc0", dst)
+    send(T.fars[:], T.H0s[:], "ars0", dst)
+
+    t0 = mm(T.pr[:, 0:P], P, "qr", 0, "H0", 0, (trc[0], trs[0], hc))
+    tu = func(T.U[:, 0:P], T.pr[:, 0:P], F.Square, t0)
+    ta = ts(T.ipm[:], T.ip[:], 15, None, A.bitwise_and, None, ti1)
+    ta = tt(T.idf[:], T.ip[:], T.ipm[:], A.subtract, ta)
+    tfc = ts(T.fc[:], T.i16[:], T.idf[:], None, A.subtract, None, ta, ti2)
+    wait("v", tfc)
+    ttg = done("v", vec.tensor_copy(T.tg[:], T.fc[:, 0:4]))
+
+    tn = tk_ = None
+    tsqa = None
+    tv1 = None
+    tyc = [None, None]
+    tyw = [None, None]
+    tsq = tu
+    late = {}
+
+    def arrived(t):
+        if t == 0:
+            return late["c0"], late["s0"]
+        return ("arc%d" % t, by(t)), ("ars%d" % t, by(t))
+
+    def products(t, tm):
+        ac, as_ = arrived(t)
+        z = [mm(T.py[:, 512 * o:512 * o + 128], 128, "wk", 128 * o, "M%d" % t, W - 128, (tw, ac, as_, ("cp%d" % t, 32), tyc[o])) for o in range(O)]
+        for o in range(O):
+            b = (t * O + o) * W
+            n = ((t + 1) * O + o) * W
+            src = T.py[:, 512 * o + 128 - K:512 * o + 128]
+            if t == R - 1 and o == 0:
+                wait("v", z[o])
+                x = done("v", vec.tensor_copy(T.yw[:, b + P:b + W], src))
+                wait("v", x, tyw[o], tm)
+                x = done("v", vec.tensor_copy(T.yw[:, n:n + P], T.yw[:, b:b + W].indirect(T.mrg[:, 16 * t:16 * t + 16])))
+            else:
+                tyc[o] = x = func(T.yw[:, b + P:b + W], src, F.Copy, z[o])
+                x = func(T.yw[:, n:n + P], T.yw[:, b:b + W].indirect(T.mrg[:, 16 * t:16 * t + 16]), F.Copy, x, tyw[o], tm)
+            tyw[o] = x
+            q = "s" if t == R - 1 and o == 1 else "y"
+            wait(q, x)
+            queue[q].dma_start(T.y[:, (t * O + o) * P:(t * O + o) * P + P], T.yw[:, n:n + P]).then_inc(T.sem.sty, 16)
+
+    tm = None
+    tw = None
+    for t in range(R):
+        H, M, S = "H%d" % t, "M%d" % t, "S%d" % t
+        last = t == R - 1
+        for h in range(2):
+            tc = mm(T.pc[:, 512 * h:512 * h + 128], 128, H, 128 * h, "qk", 0, (hc, hs, tq, tv1))
+        a = P - K if last else 0
+        wait("y", hc, hs)
+        syn.dma_start(u8(T[M][:, a:P]), u8(T[H][:, a:P])).then_inc(T.sem["cp%d" % t], 16)
+        syn.dma_start(T[M + "s"][:, a:P], T[H + "s"][:, a:P]).then_inc(T.sem["cp%d" % t], 16)
+        if t and not last:
+            tn = mm(T.pr[:, 0:P], P, "qr", 128 * (t + 1), H, 0, (trc[t + 1], trs[t + 1], tsq))
+        if t:
+            products(t - 1, tm)
+            if not last:
+                tsq = func(T.sqn[:], T.pr[:, 0:P], F.Square, tn, late["add"])
+        for h in range(2):
+            s = T.pc[:, 512 * h + t:512 * h + t + 1]
+            if t:
+                tv1 = ts(T.uc[:, h:h + 1], s, s, T.us[:, h:h + 1], A.mult, A.add, tc, late["us"])
+            else:
+                tv1 = ts(T.uc[:, h:h + 1], s, s, None, A.mult, None, tc)
+        u = t * P
+        for h in range(2):
+            x, w = 416 * h, T.uc[:, h:h + 1]
+            ts(T.X[:, x:x + 128], T.U[:, u + 128 * h:u + 128 * h + 128], w, None, A.is_equal, None, tv1, tu)
+            if h == 0:
+                ts(T.X[:, x + 128:x + 256], T.U[:, u:u + 128], w, None, A.is_le, None)
+                ts(T.X[:, x + 256:x + 384], T.U[:, u + 128:u + 256], w, None, A.is_lt, None)
+            else:
+                tx = ts(T.X[:, x + 128:x + 384], T.U[:, u:u + 256], w, None, A.is_le, None)
+        wait("v", tx, tk, tcon)
+        to = done("v", vec.tensor_tensor_scan(T.SO[:, 0:801], T.G[:, 0:801], T.X[:, 0:801], 0.0, A.mult, A.add))
+        wait("v", to)
+        for h in range(2):
+            tr = done("v", vec.transpose(T.RT[:, 32 * h:32 * h + 32], T.SO[:, 416 * h + 384:416 * h + 416]))
+        tb = []
+        for a in range(4):
+            wait("g", tr)
+            tb.append(done("g", g.partition_broadcast(T.RB[:, 64 * a:64 * a + 64], T.RT[32 * a:32 * a + 1, 0:64], 128)))
+        if not last:
+            for h in range(2):
+                late["us"] = ts(T.us[:, h:h + 1], T.SO[:, 416 * h + 384:416 * h + 385], float(K), T.uc[:, h:h + 1], A.is_ge, A.mult)
+        if t == 0:
+            x = fill(T.tab[:], 1.0)
+            fill(T.tab[:, 32:4 * P:64], 97.0, x)
+            ttab = fill(T.tab[:, 0:4 * P:64], -127.0, x)
+            trc[1] = pick("qr", "qk", 128, 256, 0, 128, off(1), (toff[1],))
+            for i in range(1, R):
+                trs[i] = picks("qrs", "qks", 128 * i, 128 * i + 128, 0, 128, off(i), (toff[i],))
+            tn = mm(T.pr[:, 0:P], P, "qr", 128, H, 0, (trc[1], trs[1], tsq))
+            tsq = func(T.sqn[:], T.pr[:, 0:P], F.Square, tn)
+        elif not last:
+            late["add"] = tt(T.V[:, t * W:t * W + P], T.U[:, u:u + P], T.sqn[:], A.add, tsq, tu)
+        for half in range(2):
+            for c in range(4):
+                tne = ts(T.NE[:, P * c + 128 * half:P * c + 128 * half + 128], T.RB[:, 128 * half:128 * half + 128], T.tg[:, c:c + 1], None, A.not_equal, None, tb[2 * half + 1], ttg)
+            if half == 0:
+                if t == 0:
+                    wait("v", ("ldw", 16))
+                    tw = done("v", vec.quantize_mx(T.wk[:], T.wks[:], T.win[:]))
+                elif t + 2 < R:
+                    i = t + 2
+                    trc[i] = pick("qr", "qk", 128 * i, 128 * i + 128, 0, 128, off(i), (toff[i],))
+        wait("v", tne, ttab)
+        tl = done("v", vec.tensor_tensor_scan(T.LO[:], T.tab[:], T.NE[:], 0.0, A.add, A.mult))
+        lst = T.lst[:, 4 * t:4 * t + 4] if t else T.lst0[:]
+        tl = ts(lst, T.LO[:, P - 1:4 * P:P], -1.0, 255.0, A.mult, A.add, tl)
+        dst = T.cores[rank ^ PART[t]]
+        if t == 0:
+            wait("g", tl)
+            send(T.lland[:], T.lst0[:], "arl", dst)
+            for o in range(O):
+                z = mm(T.py[:, 512 * o:512 * o + P], P, "wk", 128 * o, H, 0, (tw,))
+                tyw[o] = tyc[o] = func(T.yw[:, o * W:o * W + P], T.py[:, 512 * o:512 * o + P], F.Copy, z)
+        else:
+            x = pick(S, H, 0, K, 0, P, lst, (tl,))
+            z = picks(S + "s", H + "s", 0, K, 0, P, lst, (tl,))
+            wait("g", x)
+            send(u8(T[M][:, P:W]), u8(T[S][:]), "arc%d" % t, dst)
+            wait("g", z)
+            send(T[M + "s"][:, P:W], T[S + "s"][:], "ars%d" % t, dst)
+        if t == 0:
+            x = fill(T.gs[:], 1.0)
+            tgs = fill(T.gs[:, 0:P:16], 0.0, x)
+            tmk = ts(T.mk[:], T.ij[:], T.fc[:, 0:1], None, A.is_equal, None, tfc, ti3)
+        x = tt(T.mx16[:], T.RB[:], T.mk[:], A.mult, tb[3], tmk)
+        wait("v", x, tgs)
+        x = done("v", vec.tensor_tensor_scan(T.mo[:], T.gs[:], T.mx16[:], 0.0, A.mult, A.add))
+        for h in range(2):
+            for e in range(2):
+                b = 32 * h + 16 * e
+                z = ts(T.ma[:, 8 * h + e:8 * h + e + 7:2], T.mo[:, b + 15:b + 208:64], float(P), None, A.add, None, x)
+        x = ts(T.mb[:], T.ma[:], float(W), None, A.is_lt, None, z)
+        x = tt(T.mc[:], T.ma[:], T.mb[:], A.mult, x)
+        x = tt(T.md[:], T.mc[:], T.fc[:], A.max, x)
+        wait("v", x)
+        mrg = T.mrg[:, 16 * t:16 * t + 16]
+        tm = done("v", vec.tensor_copy(mrg, T.md[:]))
+        if t == 0:
+            late["add"] = tt(T.V[:, 0:P], T.U[:, 0:P], T.sqn[:], A.add, tsq, tu)
+            trc[2] = pick("qr", "qk", 256, 384, 0, 128, off(2), (toff[2],))
+            late["c0"] = pick(M, "far", P, W, 0, P, T.lland[:], (("arl", by(0)), ("arc0", by(0))))
+            late["s0"] = picks(M + "s", "fars", P, W, 0, P, T.lland[:], (("arl", by(0)), ("ars0", by(0))))
+        if not last:
+            ac, as_ = arrived(t)
+            cp = ("cp%d" % t, 32)
+            n = "H%d" % (t + 1)
+            x = mm(T.pa[:, 0:128], 128, "qr", 128 * (t + 1), M, W - 128, (ac, as_, cp, trc[t + 1], trs[t + 1], tsqa))
+            hc = pick(n, M, 0, P, 0, W, mrg, (ac, cp, tm))
+            hs = picks(n + "s", M + "s", 0, P, 0, W, mrg, (as_, cp, tm))
+            tsqa = func(T.V[:, t * W + P:t * W + W], T.pa[:, 128 - K:128], F.Square, x)
+            wait("v", late["add"], tsqa)
+            tu = done("v", vec.tensor_copy(T.U[:, u + P:u + 2 * P], T.V[:, t * W:t * W + W].indirect(mrg)))
+        else:
+            products(t, tm)
+
+    for q in ("v", "s", "p", "g"):
+        wait("y", (own[q], count[q]))
+    wait("y", ("sty", 16 * R * O))
+    wait("g", ("loc", sent[0]))

@@ -1,4 +1,3 @@
-from concourse.bass import DstId, RemoteDMATransfer
 from concourse.mybir import dt, AluOpType, ActivationFunctionType
 
 P, K, R, O = 256, 64, 6, 2
@@ -15,13 +14,12 @@ SCRATCH = {
     "wk": ("sbuf", [128, 128 * O], CODE), "wks": ("sbuf", [128, 128 * O], PLANE),
     "far": ("sbuf", [128, P], CODE), "fars": ("sbuf", [128, P], PLANE),
     "offq": ("sbuf", [128, 8 * R], "uint16"),
-    "lst0": ("sbuf", [128, K // 16], "uint16"),
-    "lland": ("sbuf", [128, K // 16], "uint16"),
     "lst": ("sbuf", [128, R * K // 16], "uint16"),
+    "lland": ("sbuf", [128, K // 16], "uint16"),
     "mrg": ("sbuf", [128, R * P // 16], "uint16"),
     "U": ("sbuf", [128, R * P], "float32"),
-    "V": ("sbuf", [128, R * W], "float32"),
     "sqn": ("sbuf", [128, P], "float32"),
+    "sqa": ("sbuf", [128, K], "float32"),
     "uc": ("sbuf", [128, 2], "float32"),
     "us": ("sbuf", [128, 2], "float32"),
     "X": ("sbuf", [128, 832], "bfloat16"),
@@ -29,13 +27,15 @@ SCRATCH = {
     "SO": ("sbuf", [128, 832], "bfloat16"),
     "RT": ("sbuf", [128, 64], "bfloat16"),
     "RB": ("sbuf", [128, P], "bfloat16"),
-    "NE": ("sbuf", [128, 4 * P], "bfloat16"),
-    "LO": ("sbuf", [128, 4 * P], "bfloat16"),
-    "tab": ("sbuf", [128, 4 * P], "bfloat16"),
-    "mk": ("sbuf", [128, P], "bfloat16"),
-    "mx16": ("sbuf", [128, P], "bfloat16"),
-    "mo": ("sbuf", [128, P], "bfloat16"),
-    "gs": ("sbuf", [128, P], "bfloat16"),
+    "ne1": ("sbuf", [128, 512], "bfloat16"),
+    "lo1": ("sbuf", [128, 512], "bfloat16"),
+    "tab1": ("sbuf", [128, 512], "bfloat16"),
+    "ne2": ("sbuf", [128, 520], "bfloat16"),
+    "lo2": ("sbuf", [128, 520], "bfloat16"),
+    "tab2": ("sbuf", [128, 520], "bfloat16"),
+    "du": ("sbuf", [128, 512], "bfloat16"),
+    "du2": ("sbuf", [128, 512], "bfloat16"),
+    "dl": ("sbuf", [128, 16], "uint16"),
     "ma": ("sbuf", [128, 16], "float32"),
     "mb": ("sbuf", [128, 16], "float32"),
     "mc": ("sbuf", [128, 16], "float32"),
@@ -46,24 +46,18 @@ SCRATCH = {
     "ip": ("sbuf", [128, 1], "int32"),
     "ipm": ("sbuf", [128, 1], "int32"),
     "idf": ("sbuf", [128, 1], "float32"),
-    "ij": ("sbuf", [128, P], "int32"),
     "yw": ("sbuf", [128, (R + 1) * O * W], "float32"),
     "pc": ("psum", [128, 1024], "float32"),
     "pa": ("psum", [128, 512], "float32"),
     "pr": ("psum", [128, 512], "float32"),
     "py": ("psum", [128, 512 * O], "float32"),
 }
+SEMAPHORES = ["sv", "ss", "sp", "sg", "ldc", "ldq", "ldw", "loc", "sty", "arl"]
 for _t in range(R):
-    SCRATCH["H%d" % _t] = ("sbuf", [128, P], CODE)
-    SCRATCH["H%ds" % _t] = ("sbuf", [128, P], PLANE)
-    SCRATCH["M%d" % _t] = ("sbuf", [128, W], CODE)
-    SCRATCH["M%ds" % _t] = ("sbuf", [128, W], PLANE)
-    if _t:
-        SCRATCH["S%d" % _t] = ("sbuf", [128, K], CODE)
-        SCRATCH["S%ds" % _t] = ("sbuf", [128, K], PLANE)
-SEMAPHORES = ["sv", "ss", "sp", "sg", "ldc", "ldq", "ldw", "loc", "arl", "sty"]
-for _t in range(R):
-    SEMAPHORES += ["cp%d" % _t, "arc%d" % _t, "ars%d" % _t]
+    for _n, _w in (("H", P), ("M", W), ("S", K)):
+        SCRATCH["%s%d" % (_n, _t)] = ("sbuf", [128, _w], CODE)
+        SCRATCH["%s%ds" % (_n, _t)] = ("sbuf", [128, _w], PLANE)
+    SEMAPHORES += [_n + str(_t) for _n in ("cp", "arc", "ars")]
 
 
 def rank_program(g, core, T, topo):
@@ -93,13 +87,14 @@ def rank_program(g, core, T, topo):
         ins.then_inc(T.sem[own[q]], 1)
         return (own[q], count[q])
 
-    def send(out_ap, in_ap, sem, dst):
+    def send(out_ap, in_ap, sem, t):
+        dst = T.cores[rank ^ PART[t]]
         rid, pid = topo.addr(dst)[:2]
         g.remote_dma(out_ap=out_ap, in_ap=in_ap, remote_sem=T.sem[sem], local_sem=T.sem["loc"], pid=pid, routing_id=rid, dma_engine_mask=topo.mask(core, dst))
         sent[0] += len(topo.engines(core, dst))
 
-    def by(t):
-        return len(topo.engines(T.cores[rank ^ PART[t]], core))
+    def came(sem, t):
+        return (sem, len(topo.engines(T.cores[rank ^ PART[t]], core)))
 
     def u8(v):
         return v.bitcast(dt.uint8)
@@ -110,7 +105,7 @@ def rank_program(g, core, T, topo):
 
     def picks(out, win, a, b, c, d, off, deps):
         wait("s", *deps)
-        return done("s", act.activation(T[out][:, a:b], T[win][:, c:d].indirect(off), F.Copy))
+        return done("s", act.activation(T[out + "s"][:, a:b], T[win + "s"][:, c:d].indirect(off), F.Copy))
 
     def mm(out, n, st, a, mv, b, deps):
         wait("p", *deps)
@@ -130,6 +125,18 @@ def rank_program(g, core, T, topo):
         wait("v", *deps)
         return done("v", vec.tensor_tensor(out, in0, in1, op))
 
+    def scan(out, d0, d1, op0, op1, *deps):
+        wait("v", *deps)
+        return done("v", vec.tensor_tensor_scan(out, d0, d1, 0.0, op0, op1))
+
+    def turn(out, in_, *deps):
+        wait("v", *deps)
+        return done("v", vec.transpose(out, in_))
+
+    def copy(out, in_, *deps):
+        wait("v", *deps)
+        return done("v", vec.tensor_copy(out, in_))
+
     def func(out, in_, f, *deps):
         wait("s", *deps)
         return done("s", act.activation(out, in_, f))
@@ -146,187 +153,174 @@ def rank_program(g, core, T, topo):
     for h in range(2):
         v = T.G[:, 416 * h:416 * h + 128]
         tk = done("g", g.affine_select(v, v, [[-1, 128]], A.not_equal, 0.0, 0, 1))
-    ti3 = done("g", g.iota(T.ij[:], [[0, 16], [1, 16]], 0, 0))
     for h in range(2):
         fill(T.G[:, 416 * h + 128:416 * h + 129], -1.0, tg1)
         fill(T.X[:, 416 * h + 384:416 * h + 416], 0.0)
-    tcon = fill(T.SO[:, 800:832], 0.0)
-    for t in range(1, R):
-        toff.append(fill(T.offq[:, 8 * t:8 * t + 8], t))
+        tcon = fill(T.SO[:, 416 * h + 384:416 * h + 416], 0.0)
+    ta = ts(T.ipm[:], T.ip[:], 15, None, A.bitwise_and, None, ti1)
+    ta = tt(T.idf[:], T.ip[:], T.ipm[:], A.subtract, ta)
+    fill(T.tab1[:], 1.0)
+    tfc = ts(T.fc[:], T.i16[:], T.idf[:], None, A.subtract, None, ta, ti2)
+    fill(T.tab2[:], 1.0)
+    for i in range(2):
+        tdl = copy(T.dl[:, i:16:2], T.fc[:, 0:8], tfc)
 
     wait("v", ("ldq", 16))
     tq = done("v", vec.quantize_mx(T.qk[:], T.qks[:], T.qin[:]))
     trc, trs = [None] * R, [None] * R
 
-    def off(t):
-        return T.offq[:, 8 * t:8 * t + 8]
+    def query(t, *deps):
+        off = T.offq[:, 8 * t:8 * t + 8]
+        trc[t] = pick("qr", "qk", 128 * t, 128 * t + 128, 0, 128, off, deps)
+        trs[t] = picks("qr", "qk", 128 * t, 128 * t + 128, 0, 128, off, deps)
 
-    trc[0] = pick("qr", "qk", 0, 128, 0, 128, off(0), (tq, toff[0]))
-    trs[0] = picks("qrs", "qks", 0, 128, 0, 128, off(0), (tq, toff[0]))
+    query(0, tq, toff[0])
     wait("v", ("ldc", 16))
-    hc = hs = done("v", vec.quantize_mx(T.H0[:], T.H0s[:], T.cin[:]))
+    x = done("v", vec.quantize_mx(T.H0[:], T.H0s[:], T.cin[:]))
+    hc = hs = [x, x]
 
-    dst = T.cores[rank ^ PART[0]]
-    wait("g", hc)
-    send(u8(T.far[:]), u8(T.H0[:]), "arc0", dst)
-    send(T.fars[:], T.H0s[:], "ars0", dst)
+    wait("g", x)
+    send(u8(T.far[:]), u8(T.H0[:]), "arc0", 0)
+    send(T.fars[:], T.H0s[:], "ars0", 0)
 
-    t0 = mm(T.pr[:, 0:P], P, "qr", 0, "H0", 0, (trc[0], trs[0], hc))
+    t0 = mm(T.pr[:, 0:P], P, "qr", 0, "H0", 0, (trc[0], trs[0], x))
     tu = func(T.U[:, 0:P], T.pr[:, 0:P], F.Square, t0)
-    ta = ts(T.ipm[:], T.ip[:], 15, None, A.bitwise_and, None, ti1)
-    ta = tt(T.idf[:], T.ip[:], T.ipm[:], A.subtract, ta)
-    tfc = ts(T.fc[:], T.i16[:], T.idf[:], None, A.subtract, None, ta, ti2)
-    wait("v", tfc)
-    ttg = done("v", vec.tensor_copy(T.tg[:], T.fc[:, 0:4]))
+    ttg = copy(T.tg[:], T.fc[:, 0:4])
+    fill(T.ne2[:, 0:520:130], 0.0)
+    ttab = fill(T.ne2[:, 1:520:130], 1.0)
+    toff += [fill(T.offq[:, 8 * i:8 * i + 8], i) for i in (1, 2)]
+    wait("v", ("ldw", 16))
+    tw = done("v", vec.quantize_mx(T.wk[:], T.wks[:], T.win[:]))
 
-    tn = tk_ = None
-    tsqa = None
-    tv1 = None
+    tsqa = tm = tadd = tus = None
+    tv = [None, None]
     tyc = [None, None]
     tyw = [None, None]
     tsq = tu
-    late = {}
-
-    def arrived(t):
-        if t == 0:
-            return late["c0"], late["s0"]
-        return ("arc%d" % t, by(t)), ("ars%d" % t, by(t))
+    arr = [(came("arc%d" % t, t), came("ars%d" % t, t)) for t in range(R)]
 
     def products(t, tm):
-        ac, as_ = arrived(t)
-        z = [mm(T.py[:, 512 * o:512 * o + 128], 128, "wk", 128 * o, "M%d" % t, W - 128, (tw, ac, as_, ("cp%d" % t, 32), tyc[o])) for o in range(O)]
+        z = [mm(T.py[:, 512 * o:512 * o + 128], 128, "wk", 128 * o, "M%d" % t, W - 128, (tw, arr[t][0], arr[t][1], ("cp%d" % t, 32), tyc[o])) for o in range(O)]
+        tail = t == R - 1
+        for o in range(O):
+            b = (t * O + o) * W
+            src = T.py[:, 512 * o + 128 - K:512 * o + 128]
+            z[o] = copy(T.yw[:, b + P:b + W], src, z[o]) if tail else z[o]
         for o in range(O):
             b = (t * O + o) * W
             n = ((t + 1) * O + o) * W
             src = T.py[:, 512 * o + 128 - K:512 * o + 128]
-            if t == R - 1 and o == 0:
-                wait("v", z[o])
-                x = done("v", vec.tensor_copy(T.yw[:, b + P:b + W], src))
-                wait("v", x, tyw[o], tm)
-                x = done("v", vec.tensor_copy(T.yw[:, n:n + P], T.yw[:, b:b + W].indirect(T.mrg[:, 16 * t:16 * t + 16])))
+            win = T.yw[:, b:b + W].indirect(T.mrg[:, 16 * t:16 * t + 16])
+            x = z[o]
+            if not tail:
+                tyc[o] = x = func(T.yw[:, b + P:b + W], src, F.Copy, x)
+            if tail and o == 0:
+                x = copy(T.yw[:, n:n + P], win, x, tyw[o], tm)
             else:
-                tyc[o] = x = func(T.yw[:, b + P:b + W], src, F.Copy, z[o])
-                x = func(T.yw[:, n:n + P], T.yw[:, b:b + W].indirect(T.mrg[:, 16 * t:16 * t + 16]), F.Copy, x, tyw[o], tm)
+                x = func(T.yw[:, n:n + P], win, F.Copy, x, tyw[o], tm)
             tyw[o] = x
-            q = "s" if t == R - 1 and o == 1 else "y"
+            q = "s" if tail and o == 1 else "y"
             wait(q, x)
             queue[q].dma_start(T.y[:, (t * O + o) * P:(t * O + o) * P + P], T.yw[:, n:n + P]).then_inc(T.sem.sty, 16)
 
-    tm = None
-    tw = None
+    def ahead(t, *deps):
+        x = mm(T.pr[:, 0:P], P, "qr", 128 * t, "H%d" % (t - 1), 0, (trc[t], trs[t], tsq))
+        return func(T.sqn[:], T.pr[:, 0:P], F.Square, x, *deps)
+
     for t in range(R):
         H, M, S = "H%d" % t, "M%d" % t, "S%d" % t
         last = t == R - 1
-        for h in range(2):
-            tc = mm(T.pc[:, 512 * h:512 * h + 128], 128, H, 128 * h, "qk", 0, (hc, hs, tq, tv1))
+        u = t * P
+        tc = [mm(T.pc[:, 512 * h:512 * h + 128], 128, H, 128 * h, "qk", 0, (hc[h], hs[h], tq, tv[h])) for h in range(2)]
         a = P - K if last else 0
-        wait("y", hc, hs)
+        wait("y", hc[1], hs[1])
         syn.dma_start(u8(T[M][:, a:P]), u8(T[H][:, a:P])).then_inc(T.sem["cp%d" % t], 16)
         syn.dma_start(T[M + "s"][:, a:P], T[H + "s"][:, a:P]).then_inc(T.sem["cp%d" % t], 16)
-        if t and not last:
-            tn = mm(T.pr[:, 0:P], P, "qr", 128 * (t + 1), H, 0, (trc[t + 1], trs[t + 1], tsq))
+        if t > 1 and not last:
+            tsq = ahead(t + 1, tadd)
+        if t == 1:
+            for o in range(O):
+                z = mm(T.py[:, 512 * o:512 * o + P], P, "wk", 128 * o, "H0", 0, (tw,))
+                tyw[o] = tyc[o] = func(T.yw[:, o * W:o * W + P], T.py[:, 512 * o:512 * o + P], F.Copy, z)
         if t:
             products(t - 1, tm)
-            if not last:
-                tsq = func(T.sqn[:], T.pr[:, 0:P], F.Square, tn, late["add"])
+        tb = []
         for h in range(2):
             s = T.pc[:, 512 * h + t:512 * h + t + 1]
-            if t:
-                tv1 = ts(T.uc[:, h:h + 1], s, s, T.us[:, h:h + 1], A.mult, A.add, tc, late["us"])
-            else:
-                tv1 = ts(T.uc[:, h:h + 1], s, s, None, A.mult, None, tc)
-        u = t * P
-        for h in range(2):
             x, w = 416 * h, T.uc[:, h:h + 1]
-            ts(T.X[:, x:x + 128], T.U[:, u + 128 * h:u + 128 * h + 128], w, None, A.is_equal, None, tv1, tu)
+            if t:
+                tv[h] = ts(w, s, s, T.us[:, h:h + 1], A.mult, A.add, tc[h], tus)
+            else:
+                tv[h] = ts(w, s, s, None, A.mult, None, tc[h])
+            ts(T.X[:, x:x + 128], T.U[:, u + 128 * h:u + 128 * h + 128], w, None, A.is_equal, None, tv[h], tu)
             if h == 0:
                 ts(T.X[:, x + 128:x + 256], T.U[:, u:u + 128], w, None, A.is_le, None)
-                ts(T.X[:, x + 256:x + 384], T.U[:, u + 128:u + 256], w, None, A.is_lt, None)
+                tx = ts(T.X[:, x + 256:x + 384], T.U[:, u + 128:u + 256], w, None, A.is_lt, None)
             else:
                 tx = ts(T.X[:, x + 128:x + 384], T.U[:, u:u + 256], w, None, A.is_le, None)
-        wait("v", tx, tk, tcon)
-        to = done("v", vec.tensor_tensor_scan(T.SO[:, 0:801], T.G[:, 0:801], T.X[:, 0:801], 0.0, A.mult, A.add))
-        wait("v", to)
-        for h in range(2):
-            tr = done("v", vec.transpose(T.RT[:, 32 * h:32 * h + 32], T.SO[:, 416 * h + 384:416 * h + 416]))
-        tb = []
-        for a in range(4):
+            to = scan(T.SO[:, x:x + 385], T.G[:, x:x + 385], T.X[:, x:x + 385], A.mult, A.add, tx, tk, tcon)
+            tr = turn(T.RT[:, 32 * h:32 * h + 32], T.SO[:, x + 384:x + 416], to)
             wait("g", tr)
-            tb.append(done("g", g.partition_broadcast(T.RB[:, 64 * a:64 * a + 64], T.RT[32 * a:32 * a + 1, 0:64], 128)))
+            for a in range(4):
+                tb.append(done("g", g.partition_broadcast(T.RB[:, 128 * h + 32 * a:128 * h + 32 * a + 32], T.RT[32 * a:32 * a + 1, 32 * h:32 * h + 32], 128)))
         if not last:
             for h in range(2):
-                late["us"] = ts(T.us[:, h:h + 1], T.SO[:, 416 * h + 384:416 * h + 385], float(K), T.uc[:, h:h + 1], A.is_ge, A.mult)
+                tus = ts(T.us[:, h:h + 1], T.SO[:, 416 * h + 384:416 * h + 385], float(K), T.uc[:, h:h + 1], A.is_ge, A.mult)
         if t == 0:
-            x = fill(T.tab[:], 1.0)
-            fill(T.tab[:, 32:4 * P:64], 97.0, x)
-            ttab = fill(T.tab[:, 0:4 * P:64], -127.0, x)
-            trc[1] = pick("qr", "qk", 128, 256, 0, 128, off(1), (toff[1],))
-            for i in range(1, R):
-                trs[i] = picks("qrs", "qks", 128 * i, 128 * i + 128, 0, 128, off(i), (toff[i],))
-            tn = mm(T.pr[:, 0:P], P, "qr", 128, H, 0, (trc[1], trs[1], tsq))
-            tsq = func(T.sqn[:], T.pr[:, 0:P], F.Square, tn)
-        elif not last:
-            late["add"] = tt(T.V[:, t * W:t * W + P], T.U[:, u:u + P], T.sqn[:], A.add, tsq, tu)
-        for half in range(2):
-            for c in range(4):
-                tne = ts(T.NE[:, P * c + 128 * half:P * c + 128 * half + 128], T.RB[:, 128 * half:128 * half + 128], T.tg[:, c:c + 1], None, A.not_equal, None, tb[2 * half + 1], ttg)
-            if half == 0:
-                if t == 0:
-                    wait("v", ("ldw", 16))
-                    tw = done("v", vec.quantize_mx(T.wk[:], T.wks[:], T.win[:]))
-                elif t + 2 < R:
-                    i = t + 2
-                    trc[i] = pick("qr", "qk", 128 * i, 128 * i + 128, 0, 128, off(i), (toff[i],))
-        wait("v", tne, ttab)
-        tl = done("v", vec.tensor_tensor_scan(T.LO[:], T.tab[:], T.NE[:], 0.0, A.add, A.mult))
-        lst = T.lst[:, 4 * t:4 * t + 4] if t else T.lst0[:]
-        tl = ts(lst, T.LO[:, P - 1:4 * P:P], -1.0, 255.0, A.mult, A.add, tl)
-        dst = T.cores[rank ^ PART[t]]
+            query(1, toff[1])
+            tsq = ahead(1)
+            trs[2] = picks("qr", "qk", 256, 384, 0, 128, T.offq[:, 16:24], (toff[2],))
+        if t == 1:
+            trc[2] = pick("qr", "qk", 256, 384, 0, 128, T.offq[:, 16:24], (toff[2],))
+        td = [func(T.du[:, 256 * h:256 * h + 256], T.RB[:, 128 * h:128 * h + 128].indirect(T.dl[:]), F.Copy, tb[4 * h + 3], tdl) for h in range(2)]
+        for c in range(4):
+            x = ts(T.ne1[:, 128 * c:128 * c + 128], T.RB[:, 0:128], T.tg[:, c:c + 1], None, A.not_equal, None, tb[3], ttg)
+        x = scan(T.lo1[:], T.tab1[:], T.ne1[:], A.add, A.mult, x, ttab)
+        copy(T.tab2[:, 1:520:130], T.lo1[:, 127:512:128], x)
+        for c in range(4):
+            x = ts(T.ne2[:, 130 * c + 2:130 * c + 130], T.RB[:, 128:256], T.tg[:, c:c + 1], None, A.not_equal, None, tb[7])
+        x = scan(T.lo2[:], T.tab2[:], T.ne2[:], A.add, A.mult, x)
+        lst = T.lst[:, 4 * t:4 * t + 4]
+        tl = ts(lst, T.lo2[:, 129:520:130], -1.0, 255.0, A.mult, A.add, x)
         if t == 0:
             wait("g", tl)
-            send(T.lland[:], T.lst0[:], "arl", dst)
-            for o in range(O):
-                z = mm(T.py[:, 512 * o:512 * o + P], P, "wk", 128 * o, H, 0, (tw,))
-                tyw[o] = tyc[o] = func(T.yw[:, o * W:o * W + P], T.py[:, 512 * o:512 * o + P], F.Copy, z)
+            send(T.lland[:], lst, "arl", t)
         else:
             x = pick(S, H, 0, K, 0, P, lst, (tl,))
-            z = picks(S + "s", H + "s", 0, K, 0, P, lst, (tl,))
+            z = picks(S, H, 0, K, 0, P, lst, (tl,))
             wait("g", x)
-            send(u8(T[M][:, P:W]), u8(T[S][:]), "arc%d" % t, dst)
+            send(u8(T[M][:, P:W]), u8(T[S][:]), "arc%d" % t, t)
             wait("g", z)
-            send(T[M + "s"][:, P:W], T[S + "s"][:], "ars%d" % t, dst)
-        if t == 0:
-            x = fill(T.gs[:], 1.0)
-            tgs = fill(T.gs[:, 0:P:16], 0.0, x)
-            tmk = ts(T.mk[:], T.ij[:], T.fc[:, 0:1], None, A.is_equal, None, tfc, ti3)
-        x = tt(T.mx16[:], T.RB[:], T.mk[:], A.mult, tb[3], tmk)
-        wait("v", x, tgs)
-        x = done("v", vec.tensor_tensor_scan(T.mo[:], T.gs[:], T.mx16[:], 0.0, A.mult, A.add))
-        for h in range(2):
-            for e in range(2):
-                b = 32 * h + 16 * e
-                z = ts(T.ma[:, 8 * h + e:8 * h + e + 7:2], T.mo[:, b + 15:b + 208:64], float(P), None, A.add, None, x)
-        x = ts(T.mb[:], T.ma[:], float(W), None, A.is_lt, None, z)
+            send(T[M + "s"][:, P:W], T[S + "s"][:], "ars%d" % t, t)
+        if t == 1:
+            tsq = ahead(2, tadd)
+        x = turn(T.du2[:], T.du[:], *td)
+        ts(T.ma[:], T.du2[:, 0:512:32], float(P), None, A.add, None, x)
+        x = ts(T.mb[:], T.du2[:, 0:512:32], float(K), None, A.is_lt, None)
         x = tt(T.mc[:], T.ma[:], T.mb[:], A.mult, x)
         x = tt(T.md[:], T.mc[:], T.fc[:], A.max, x)
-        wait("v", x)
         mrg = T.mrg[:, 16 * t:16 * t + 16]
-        tm = done("v", vec.tensor_copy(mrg, T.md[:]))
-        if t == 0:
-            late["add"] = tt(T.V[:, 0:P], T.U[:, 0:P], T.sqn[:], A.add, tsq, tu)
-            trc[2] = pick("qr", "qk", 256, 384, 0, 128, off(2), (toff[2],))
-            late["c0"] = pick(M, "far", P, W, 0, P, T.lland[:], (("arl", by(0)), ("arc0", by(0))))
-            late["s0"] = picks(M + "s", "fars", P, W, 0, P, T.lland[:], (("arl", by(0)), ("ars0", by(0))))
+        tm = copy(mrg, T.md[:], x)
         if not last:
-            ac, as_ = arrived(t)
+            tadd = tt(T.U[:, u + P:u + 2 * P], T.U[:, u:u + P], T.sqn[:], A.add, tsq, tu)
+        if t and t + 2 < R:
+            query(t + 2, fill(T.offq[:, 8 * t + 16:8 * t + 24], t + 2))
+        if t == 0:
+            z = came("arl", t)
+            arr[t] = (pick(M, "far", P, W, 0, P, T.lland[:], (z, arr[t][0])), picks(M, "far", P, W, 0, P, T.lland[:], (z, arr[t][1])))
+        if not last:
+            ac, as_ = arr[t]
             cp = ("cp%d" % t, 32)
             n = "H%d" % (t + 1)
-            x = mm(T.pa[:, 0:128], 128, "qr", 128 * (t + 1), M, W - 128, (ac, as_, cp, trc[t + 1], trs[t + 1], tsqa))
-            hc = pick(n, M, 0, P, 0, W, mrg, (ac, cp, tm))
-            hs = picks(n + "s", M + "s", 0, P, 0, W, mrg, (as_, cp, tm))
-            tsqa = func(T.V[:, t * W + P:t * W + W], T.pa[:, 128 - K:128], F.Square, x)
-            wait("v", late["add"], tsqa)
-            tu = done("v", vec.tensor_copy(T.U[:, u + P:u + 2 * P], T.V[:, t * W:t * W + W].indirect(mrg)))
+            z = mm(T.pa[:, 0:128], 128, "qr", 128 * (t + 1), M, W - 128, (ac, as_, cp, trc[t + 1], trs[t + 1], tsqa))
+            hc, hs = [], []
+            for h in range(2):
+                off = T.mrg[:, 16 * t + 8 * h:16 * t + 8 * h + 8]
+                hc.append(pick(n, M, 128 * h, 128 * h + 128, 0, W, off, (ac, cp, tm)))
+                hs.append(picks(n, M, 128 * h, 128 * h + 128, 0, W, off, (as_, cp, tm)))
+                if h == 0:
+                    tsqa = func(T.sqa[:], T.pa[:, 128 - K:128], F.Square, z, tu)
+            tu = copy(T.U[:, u + P:u + 2 * P].indirect(lst), T.sqa[:], tadd, tsqa)
         else:
             products(t, tm)
 

@@ -245,27 +245,47 @@ def rank_program(g, core, T, topo):
         if t:
             products(t - 1, tm)
         tb = []
-        for h in range(2):
+        uses = [T.uc[:, h:h + 1] for h in range(2)]
+
+        def use(h):
             s = T.pc[:, 512 * h + t:512 * h + t + 1]
-            x, w = 416 * h, T.uc[:, h:h + 1]
             if t:
-                tv[h] = ts(w, s, s, T.us[:, h:h + 1], A.mult, A.add, tc[h], tus)
+                tv[h] = ts(uses[h], s, s, T.us[:, h:h + 1], A.mult, A.add, tc[h], tus_old)
             else:
-                tv[h] = ts(w, s, s, None, A.mult, None, tc[h])
-            ts(T.X[:, x:x + 128], T.U[:, u + 128 * h:u + 128 * h + 128], w, None, A.is_equal, None, tv[h], tu)
-            if h == 0:
-                ts(T.X[:, x + 128:x + 256], T.U[:, u:u + 128], w, None, A.is_le, None)
-                tx = ts(T.X[:, x + 256:x + 384], T.U[:, u + 128:u + 256], w, None, A.is_lt, None)
-            else:
-                tx = ts(T.X[:, x + 128:x + 384], T.U[:, u:u + 256], w, None, A.is_le, None)
-            to = scan(T.SO[:, x:x + 385], T.G[:, x:x + 385], T.X[:, x:x + 385], A.mult, A.add, tx, tk, tcon)
-            tr = turn(T.RT[:, 32 * h:32 * h + 32], T.SO[:, x + 384:x + 416], to)
+                tv[h] = ts(uses[h], s, s, None, A.mult, None, tc[h])
+
+        def equal(h):
+            return ts(T.X[:, 416 * h:416 * h + 128], T.U[:, u + 128 * h:u + 128 * h + 128], uses[h], None, A.is_equal, None, tv[h], tu)
+
+        def add_up(h, tx):
+            x = 416 * h
+            return scan(T.SO[:, x:x + 385], T.G[:, x:x + 385], T.X[:, x:x + 385], A.mult, A.add, tx, tk, tcon)
+
+        def spread(h, to):
+            tr = turn(T.RT[:, 32 * h:32 * h + 32], T.SO[:, 416 * h + 384:416 * h + 416], to)
             wait("g", tr)
             for a in range(4):
                 tb.append(done("g", g.partition_broadcast(T.RB[:, 128 * h + 32 * a:128 * h + 32 * a + 32], T.RT[32 * a:32 * a + 1, 32 * h:32 * h + 32], 128)))
+
+        def keep(h, to):
+            return ts(T.us[:, h:h + 1], T.SO[:, 416 * h + 384:416 * h + 385], float(K), uses[h], A.is_ge, A.mult, to)
+
+        tus_old = tus
+        use(0)
+        equal(0)
+        ts(T.X[:, 128:256], T.U[:, u:u + 128], uses[0], None, A.is_le, None)
+        tx = ts(T.X[:, 256:384], T.U[:, u + 128:u + 256], uses[0], None, A.is_lt, None)
+        use(1)
+        to = add_up(0, tx)
+        equal(1)
+        spread(0, to)
+        tx = ts(T.X[:, 416 + 128:416 + 384], T.U[:, u:u + 256], uses[1], None, A.is_le, None)
         if not last:
-            for h in range(2):
-                tus = ts(T.us[:, h:h + 1], T.SO[:, 416 * h + 384:416 * h + 385], float(K), T.uc[:, h:h + 1], A.is_ge, A.mult)
+            keep(0, to)
+        to = add_up(1, tx)
+        spread(1, to)
+        if not last:
+            tus = keep(1, to)
         if t == 0:
             query(1, toff[1])
             tsq = ahead(1)
@@ -276,10 +296,10 @@ def rank_program(g, core, T, topo):
         for c in range(4):
             x = ts(T.ne1[:, 128 * c:128 * c + 128], T.RB[:, 0:128], T.tg[:, c:c + 1], None, A.not_equal, None, tb[3], ttg)
         x = scan(T.lo1[:], T.tab1[:], T.ne1[:], A.add, A.mult, x, ttab)
-        copy(T.tab2[:, 1:520:130], T.lo1[:, 127:512:128], x)
-        for c in range(4):
-            x = ts(T.ne2[:, 130 * c + 2:130 * c + 130], T.RB[:, 128:256], T.tg[:, c:c + 1], None, A.not_equal, None, tb[7])
-        x = scan(T.lo2[:], T.tab2[:], T.ne2[:], A.add, A.mult, x)
+        z = copy(T.tab2[:, 1:520:130], T.lo1[:, 127:512:128], x)
+        x = [ts(T.ne2[:, 130 * c + 2:130 * c + 130], T.RB[:, 128:256], T.tg[:, c:c + 1], None, A.not_equal, None, tb[7]) for c in range(4)]
+        scan(T.lo2[:, 0:260], T.tab2[:, 0:260], T.ne2[:, 0:260], A.add, A.mult, x[1], z)
+        x = scan(T.lo2[:, 260:520], T.tab2[:, 260:520], T.ne2[:, 260:520], A.add, A.mult, x[3])
         lst = T.lst[:, 4 * t:4 * t + 4]
         tl = ts(lst, T.lo2[:, 129:520:130], -1.0, 255.0, A.mult, A.add, x)
         if t == 0:

from concourse.mybir import dt, AluOpType, ActivationFunctionType

P, K, R, O = 256, 64, 6, 2
PART = [1, 2, 1, 2, 1, 2]
W = P + K
CODE, PLANE = "float8_e4m3fn_x4", "uint8"

SCRATCH = {
    "cin": ("sbuf", [128, 4 * P], "bfloat16"),
    "qin": ("sbuf", [128, 512], "bfloat16"),
    "win": ("sbuf", [128, 512 * O], "bfloat16"),
    "qk": ("sbuf", [128, 128], CODE), "qks": ("sbuf", [128, 128], PLANE),
    "qr": ("sbuf", [128, 128 * R], CODE), "qrs": ("sbuf", [128, 128 * R], PLANE),
    "wk": ("sbuf", [128, 128 * O], CODE), "wks": ("sbuf", [128, 128 * O], PLANE),
    "far": ("sbuf", [128, P], CODE), "fars": ("sbuf", [128, P], PLANE),
    "offq": ("sbuf", [128, 8 * R], "uint16"),
    "lst": ("sbuf", [128, R * K // 16], "uint16"),
    "lland": ("sbuf", [128, K // 16], "uint16"),
    "mrg": ("sbuf", [128, R * P // 16], "uint16"),
    "U": ("sbuf", [128, R * P], "float32"),
    "sqn": ("sbuf", [128, P], "float32"),
    "sqa": ("sbuf", [128, K], "float32"),
    "uc": ("sbuf", [128, 2], "float32"),
    "us": ("sbuf", [128, 2], "float32"),
    "X": ("sbuf", [128, 832], "bfloat16"),
    "G": ("sbuf", [128, 832], "bfloat16"),
    "SO": ("sbuf", [128, 832], "bfloat16"),
    "RT": ("sbuf", [128, 64], "bfloat16"),
    "RB": ("sbuf", [128, P], "bfloat16"),
    "ne1": ("sbuf", [128, 512], "bfloat16"),
    "lo1": ("sbuf", [128, 512], "bfloat16"),
    "tab1": ("sbuf", [128, 512], "bfloat16"),
    "ne2": ("sbuf", [128, 520], "bfloat16"),
    "lo2": ("sbuf", [128, 520], "bfloat16"),
    "tab2": ("sbuf", [128, 520], "bfloat16"),
    "du": ("sbuf", [128, 512], "bfloat16"),
    "du2": ("sbuf", [128, 512], "bfloat16"),
    "dl": ("sbuf", [128, 16], "uint16"),
    "ma": ("sbuf", [128, 16], "float32"),
    "mb": ("sbuf", [128, 16], "float32"),
    "mc": ("sbuf", [128, 16], "float32"),
    "md": ("sbuf", [128, 16], "float32"),
    "fc": ("sbuf", [128, 16], "float32"),
    "tg": ("sbuf", [128, 4], "bfloat16"),
    "i16": ("sbuf", [128, 16], "int32"),
    "ip": ("sbuf", [128, 1], "int32"),
    "ipm": ("sbuf", [128, 1], "int32"),
    "idf": ("sbuf", [128, 1], "float32"),
    "yw": ("sbuf", [128, (R + 1) * O * W], "float32"),
    "pc": ("psum", [128, 1024], "float32"),
    "pa": ("psum", [128, 512], "float32"),
    "pr": ("psum", [128, 512], "float32"),
    "py": ("psum", [128, 512 * O], "float32"),
}
SEMAPHORES = ["sv", "ss", "sp", "sg", "ldc", "ldq", "ldw", "loc", "sty", "arl"]
for _t in range(R):
    for _n, _w in (("H", P), ("M", W), ("S", K)):
        SCRATCH["%s%d" % (_n, _t)] = ("sbuf", [128, _w], CODE)
        SCRATCH["%s%ds" % (_n, _t)] = ("sbuf", [128, _w], PLANE)
    SEMAPHORES += [_n + str(_t) for _n in ("cp", "arc", "ars")]


def rank_program(g, core, T, topo):
    rank = T.rank_of(core)
    if rank is None:
        return
    A, F = AluOpType, ActivationFunctionType
    vec, act, ten, syn = g.vector, g.scalar, g.tensor, g.sync
    queue = {"v": vec, "s": act, "p": ten, "g": g, "y": syn}
    count = {"v": 0, "s": 0, "p": 0, "g": 0}
    own = {"v": "sv", "s": "ss", "p": "sp", "g": "sg"}
    seen = {}
    sent = [0]

    def wait(q, *deps):
        top = {}
        for d in deps:
            if d is not None:
                top[d[0]] = max(top.get(d[0], 0), d[1])
        for s in top:
            if seen.get((q, s), 0) < top[s]:
                queue[q].wait_ge(T.sem[s], top[s])
                seen[(q, s)] = top[s]

    def done(q, ins):
        count[q] += 1
        ins.then_inc(T.sem[own[q]], 1)
        return (own[q], count[q])

    def send(out_ap, in_ap, sem, t):
        dst = T.cores[rank ^ PART[t]]
        rid, pid = topo.addr(dst)[:2]
        g.remote_dma(out_ap=out_ap, in_ap=in_ap, remote_sem=T.sem[sem], local_sem=T.sem["loc"], pid=pid, routing_id=rid, dma_engine_mask=topo.mask(core, dst))
        sent[0] += len(topo.engines(core, dst))

    def came(sem, t):
        return (sem, len(topo.engines(T.cores[rank ^ PART[t]], core)))

    def u8(v):
        return v.bitcast(dt.uint8)

    def pick(out, win, a, b, c, d, off, deps):
        wait("v", *deps)
        return done("v", vec.tensor_copy(T[out][:, a:b].bitcast(dt.uint32), T[win][:, c:d].bitcast(dt.uint32).indirect(off)))

    def picks(out, win, a, b, c, d, off, deps):
        wait("s", *deps)
        return done("s", act.activation(T[out + "s"][:, a:b], T[win + "s"][:, c:d].indirect(off), F.Copy))

    def mm(out, n, st, a, mv, b, deps):
        wait("p", *deps)
        return done("p", ten.matmul_mx(out, T[st][:, a:a + 128], T[st + "s"][:, a:a + 128], T[mv][:, b:b + n], T[mv + "s"][:, b:b + n], True, True))

    def fill(ap, x, *deps):
        wait("v", *deps)
        return done("v", vec.memset(ap, x))

    def ts(out, in0, s1, s2, op0, op1, *deps):
        wait("v", *deps)
        if op1 is None:
            return done("v", vec.tensor_scalar(out, in0, s1, None, op0))
        return done("v", vec.tensor_scalar(out, in0, s1, s2, op0, op1))

    def tt(out, in0, in1, op, *deps):
        wait("v", *deps)
        return done("v", vec.tensor_tensor(out, in0, in1, op))

    def scan(out, d0, d1, op0, op1, *deps):
        wait("v", *deps)
        return done("v", vec.tensor_tensor_scan(out, d0, d1, 0.0, op0, op1))

    def turn(out, in_, *deps):
        wait("v", *deps)
        return done("v", vec.transpose(out, in_))

    def copy(out, in_, *deps):
        wait("v", *deps)
        return done("v", vec.tensor_copy(out, in_))

    def func(out, in_, f, *deps):
        wait("s", *deps)
        return done("s", act.activation(out, in_, f))

    act.dma_start(T.qin[:], T.qt[:]).then_inc(T.sem.ldq, 16)
    syn.dma_start(T.cin[:], T.c[:]).then_inc(T.sem.ldc, 16)
    syn.dma_start(T.win[:], T.w[:]).then_inc(T.sem.ldw, 16)
    toff = [fill(T.offq[:, 0:8], 0)]
    tg1 = fill(T.G[:], 1.0)
    ti1 = done("g", g.iota(T.ip[:], [[1, 1]], 0, 1))
    ti2 = done("g", g.iota(T.i16[:], [[16, 16]], 0, 1))
    wait("g", tg1)
    tk = None
    for h in range(2):
        v = T.G[:, 416 * h:416 * h + 128]
        tk = done("g", g.affine_select(v, v, [[-1, 128]], A.not_equal, 0.0, 0, 1))
    for h in range(2):
        fill(T.G[:, 416 * h + 128:416 * h + 129], -1.0, tg1)
        fill(T.X[:, 416 * h + 384:416 * h + 416], 0.0)
        tcon = fill(T.SO[:, 416 * h + 384:416 * h + 416], 0.0)
    ta = ts(T.ipm[:], T.ip[:], 15, None, A.bitwise_and, None, ti1)
    ta = tt(T.idf[:], T.ip[:], T.ipm[:], A.subtract, ta)
    fill(T.tab1[:], 1.0)
    tfc = ts(T.fc[:], T.i16[:], T.idf[:], None, A.subtract, None, ta, ti2)
    fill(T.tab2[:], 1.0)
    for i in range(2):
        tdl = copy(T.dl[:, i:16:2], T.fc[:, 0:8], tfc)

    wait("v", ("ldq", 16))
    tq = done("v", vec.quantize_mx(T.qk[:], T.qks[:], T.qin[:]))
    trc, trs = [None] * R, [None] * R

    def query(t, *deps):
        off = T.offq[:, 8 * t:8 * t + 8]
        trc[t] = pick("qr", "qk", 128 * t, 128 * t + 128, 0, 128, off, deps)
        trs[t] = picks("qr", "qk", 128 * t, 128 * t + 128, 0, 128, off, deps)

    query(0, tq, toff[0])
    wait("v", ("ldc", 16))
    x = done("v", vec.quantize_mx(T.H0[:], T.H0s[:], T.cin[:]))
    hc = hs = [x, x]

    wait("g", x)
    send(u8(T.far[:]), u8(T.H0[:]), "arc0", 0)
    send(T.fars[:], T.H0s[:], "ars0", 0)

    t0 = mm(T.pr[:, 0:P], P, "qr", 0, "H0", 0, (trc[0], trs[0], x))
    tu = func(T.U[:, 0:P], T.pr[:, 0:P], F.Square, t0)
    ttg = copy(T.tg[:], T.fc[:, 0:4])
    fill(T.ne2[:, 0:520:130], 0.0)
    ttab = fill(T.ne2[:, 1:520:130], 1.0)
    toff += [fill(T.offq[:, 8 * i:8 * i + 8], i) for i in (1, 2)]
    wait("v", ("ldw", 16))
    tw = done("v", vec.quantize_mx(T.wk[:], T.wks[:], T.win[:]))

    tsqa = tm = tadd = tus = None
    tv = [None, None]
    tyc = [None, None]
    tyw = [None, None]
    tsq = tu
    arr = [(came("arc%d" % t, t), came("ars%d" % t, t)) for t in range(R)]

    def products(t, tm):
        z = [mm(T.py[:, 512 * o:512 * o + 128], 128, "wk", 128 * o, "M%d" % t, W - 128, (tw, arr[t][0], arr[t][1], ("cp%d" % t, 32), tyc[o])) for o in range(O)]
        tail = t == R - 1
        for o in range(O):
            b = (t * O + o) * W
            src = T.py[:, 512 * o + 128 - K:512 * o + 128]
            z[o] = copy(T.yw[:, b + P:b + W], src, z[o]) if tail else z[o]
        for o in range(O):
            b = (t * O + o) * W
            n = ((t + 1) * O + o) * W
            src = T.py[:, 512 * o + 128 - K:512 * o + 128]
            win = T.yw[:, b:b + W].indirect(T.mrg[:, 16 * t:16 * t + 16])
            x = z[o]
            if not tail:
                tyc[o] = x = func(T.yw[:, b + P:b + W], src, F.Copy, x)
            if tail and o == 0:
                x = copy(T.yw[:, n:n + P], win, x, tyw[o], tm)
            else:
                x = func(T.yw[:, n:n + P], win, F.Copy, x, tyw[o], tm)
            tyw[o] = x
            q = "s" if tail and o == 1 else "y"
            wait(q, x)
            queue[q].dma_start(T.y[:, (t * O + o) * P:(t * O + o) * P + P], T.yw[:, n:n + P]).then_inc(T.sem.sty, 16)

    def ahead(t, *deps):
        x = mm(T.pr[:, 0:P], P, "qr", 128 * t, "H%d" % (t - 1), 0, (trc[t], trs[t], tsq))
        return func(T.sqn[:], T.pr[:, 0:P], F.Square, x, *deps)

    for t in range(R):
        H, M, S = "H%d" % t, "M%d" % t, "S%d" % t
        last = t == R - 1
        u = t * P
        tc = [mm(T.pc[:, 512 * h:512 * h + 128], 128, H, 128 * h, "qk", 0, (hc[h], hs[h], tq, tv[h])) for h in range(2)]
        a = P - K if last else 0
        wait("y", hc[1], hs[1])
        syn.dma_start(u8(T[M][:, a:P]), u8(T[H][:, a:P])).then_inc(T.sem["cp%d" % t], 16)
        syn.dma_start(T[M + "s"][:, a:P], T[H + "s"][:, a:P]).then_inc(T.sem["cp%d" % t], 16)
        if t > 1 and not last:
            tsq = ahead(t + 1, tadd)
        if t == 1:
            for o in range(O):
                z = mm(T.py[:, 512 * o:512 * o + P], P, "wk", 128 * o, "H0", 0, (tw,))
                tyw[o] = tyc[o] = func(T.yw[:, o * W:o * W + P], T.py[:, 512 * o:512 * o + P], F.Copy, z)
        if t:
            products(t - 1, tm)
        tb = []
        uses = [T.uc[:, h:h + 1] for h in range(2)]

        def use(h):
            s = T.pc[:, 512 * h + t:512 * h + t + 1]
            if t:
                tv[h] = ts(uses[h], s, s, T.us[:, h:h + 1], A.mult, A.add, tc[h], tus_old)
            else:
                tv[h] = ts(uses[h], s, s, None, A.mult, None, tc[h])

        def equal(h):
            return ts(T.X[:, 416 * h:416 * h + 128], T.U[:, u + 128 * h:u + 128 * h + 128], uses[h], None, A.is_equal, None, tv[h], tu)

        def add_up(h, tx):
            x = 416 * h
            return scan(T.SO[:, x:x + 385], T.G[:, x:x + 385], T.X[:, x:x + 385], A.mult, A.add, tx, tk, tcon)

        def spread(h, to):
            tr = turn(T.RT[:, 32 * h:32 * h + 32], T.SO[:, 416 * h + 384:416 * h + 416], to)
            wait("g", tr)
            for a in range(4):
                tb.append(done("g", g.partition_broadcast(T.RB[:, 128 * h + 32 * a:128 * h + 32 * a + 32], T.RT[32 * a:32 * a + 1, 32 * h:32 * h + 32], 128)))

        def keep(h, to):
            return ts(T.us[:, h:h + 1], T.SO[:, 416 * h + 384:416 * h + 385], float(K), uses[h], A.is_ge, A.mult, to)

        tus_old = tus
        use(0)
        equal(0)
        ts(T.X[:, 128:256], T.U[:, u:u + 128], uses[0], None, A.is_le, None)
        tx = ts(T.X[:, 256:384], T.U[:, u + 128:u + 256], uses[0], None, A.is_lt, None)
        use(1)
        to = add_up(0, tx)
        equal(1)
        spread(0, to)
        tx = ts(T.X[:, 416 + 128:416 + 384], T.U[:, u:u + 256], uses[1], None, A.is_le, None)
        if not last:
            keep(0, to)
        to = add_up(1, tx)
        spread(1, to)
        if not last:
            tus = keep(1, to)
        if t == 0:
            query(1, toff[1])
            tsq = ahead(1)
            trs[2] = picks("qr", "qk", 256, 384, 0, 128, T.offq[:, 16:24], (toff[2],))
        if t == 1:
            trc[2] = pick("qr", "qk", 256, 384, 0, 128, T.offq[:, 16:24], (toff[2],))
        td = [func(T.du[:, 256 * h:256 * h + 256], T.RB[:, 128 * h:128 * h + 128].indirect(T.dl[:]), F.Copy, tb[4 * h + 3], tdl) for h in range(2)]
        for c in range(4):
            x = ts(T.ne1[:, 128 * c:128 * c + 128], T.RB[:, 0:128], T.tg[:, c:c + 1], None, A.not_equal, None, tb[3], ttg)
        x = scan(T.lo1[:], T.tab1[:], T.ne1[:], A.add, A.mult, x, ttab)
        z = copy(T.tab2[:, 1:520:130], T.lo1[:, 127:512:128], x)
        x = [ts(T.ne2[:, 130 * c + 2:130 * c + 130], T.RB[:, 128:256], T.tg[:, c:c + 1], None, A.not_equal, None, tb[7]) for c in range(4)]
        scan(T.lo2[:, 0:260], T.tab2[:, 0:260], T.ne2[:, 0:260], A.add, A.mult, x[1], z)
        x = scan(T.lo2[:, 260:520], T.tab2[:, 260:520], T.ne2[:, 260:520], A.add, A.mult, x[3])
        lst = T.lst[:, 4 * t:4 * t + 4]
        tl = ts(lst, T.lo2[:, 129:520:130], -1.0, 255.0, A.mult, A.add, x)
        if t == 0:
            wait("g", tl)
            send(T.lland[:], lst, "arl", t)
        else:
            x = pick(S, H, 0, K, 0, P, lst, (tl,))
            z = picks(S, H, 0, K, 0, P, lst, (tl,))
            wait("g", x)
            send(u8(T[M][:, P:W]), u8(T[S][:]), "arc%d" % t, t)
            wait("g", z)
            send(T[M + "s"][:, P:W], T[S + "s"][:], "ars%d" % t, t)
        if t == 1:
            tsq = ahead(2, tadd)
        x = turn(T.du2[:], T.du[:], *td)
        ts(T.ma[:], T.du2[:, 0:512:32], float(P), None, A.add, None, x)
        x = ts(T.mb[:], T.du2[:, 0:512:32], float(K), None, A.is_lt, None)
        x = tt(T.mc[:], T.ma[:], T.mb[:], A.mult, x)
        x = tt(T.md[:], T.mc[:], T.fc[:], A.max, x)
        mrg = T.mrg[:, 16 * t:16 * t + 16]
        tm = copy(mrg, T.md[:], x)
        if not last:
            tadd = tt(T.U[:, u + P:u + 2 * P], T.U[:, u:u + P], T.sqn[:], A.add, tsq, tu)
        if t and t + 2 < R:
            query(t + 2, fill(T.offq[:, 8 * t + 16:8 * t + 24], t + 2))
        if t == 0:
            z = came("arl", t)
            arr[t] = (pick(M, "far", P, W, 0, P, T.lland[:], (z, arr[t][0])), picks(M, "far", P, W, 0, P, T.lland[:], (z, arr[t][1])))
        if not last:
            ac, as_ = arr[t]
            cp = ("cp%d" % t, 32)
            n = "H%d" % (t + 1)
            z = mm(T.pa[:, 0:128], 128, "qr", 128 * (t + 1), M, W - 128, (ac, as_, cp, trc[t + 1], trs[t + 1], tsqa))
            hc, hs = [], []
            for h in range(2):
                off = T.mrg[:, 16 * t + 8 * h:16 * t + 8 * h + 8]
                hc.append(pick(n, M, 128 * h, 128 * h + 128, 0, W, off, (ac, cp, tm)))
                hs.append(picks(n, M, 128 * h, 128 * h + 128, 0, W, off, (as_, cp, tm)))
                if h == 0:
                    tsqa = func(T.sqa[:], T.pa[:, 128 - K:128], F.Square, z, tu)
            tu = copy(T.U[:, u + P:u + 2 * P].indirect(lst), T.sqa[:], tadd, tsqa)
        else:
            products(t, tm)

    for q in ("v", "s", "p", "g"):
        wait("y", (own[q], count[q]))
    wait("y", ("sty", 16 * R * O))
    wait("g", ("loc", sent[0]))
